import numpy as np
import ml_dtypes


def mxq(x, axis, fmt="e4m3"):
    dtype, down = {"e4m3": (ml_dtypes.float8_e4m3fn, 7), "e5m2": (ml_dtypes.float8_e5m2, 14)}[fmt]
    v = np.moveaxis(np.asarray(x, np.float32).astype(ml_dtypes.bfloat16).astype(np.float64), axis, -1)
    blocks = v.reshape(v.shape[:-1] + (-1, 32))
    amax = np.abs(blocks).max(-1, keepdims=True)
    byte = np.maximum(np.where(amax > 0, np.frexp(amax)[1] - 1 + 127, 0) - down, 1)
    scale = np.exp2(byte - 127.0)
    codes = (blocks / scale).astype(np.float32).astype(dtype).astype(np.float64)
    return np.moveaxis((codes * scale).reshape(v.shape), -1, axis)


WIDE = False


def mx_kscale(k):
    if not WIDE:
        return np.ones(k)
    levels = np.array([10, -10, 5, -5, 0])
    if k % 512:
        return np.exp2(np.random.permutation(np.resize(levels, k // 32))).repeat(32)
    a = np.empty((k // 512, 16))
    for p in range(k // 512):
        a[p, :8] = np.random.permutation(np.resize(levels, 8))
        for g in range(8):
            far = levels[np.abs(levels - a[p, g]) >= 10]
            a[p, g + 8] = far[np.random.randint(len(far))]
    return np.exp2(a.ravel()).repeat(32)


def f64(x):
    return np.asarray(x).astype(np.float64)


def striped(idx):
    return np.tile(np.asarray(idx).reshape(-1, 16).T, (8, 1)).astype(np.uint16)


def unstriped(offs):
    return offs[:16].T.reshape(-1).astype(np.int64)


E2M1 = np.array([0.0, 0.5, 1.0, 1.5, 2.0, 3.0, 4.0, 6.0, -0.0, -0.5, -1.0, -1.5, -2.0, -3.0, -4.0, -6.0])


def pack_weight(w, fmt):
    k, n = w.shape
    w = f64(np.asarray(w, np.float32).astype(ml_dtypes.bfloat16)).reshape(k // 32, 32, n)
    amax = np.abs(w).max(1)
    if fmt == "e4m3":
        byte = np.frexp(amax)[1] - 1 + 127 - 7
    else:
        mant, ex = np.frexp(amax / 6.0)
        byte = np.where(mant > 0.5, ex, ex - 1) + 127
    byte = np.clip(np.where(amax > 0, byte, 1), 1, 254)
    scaled = (w * np.exp2(127.0 - byte)[:, None, :]).reshape(k, n).astype(np.float32)
    by_word = np.ascontiguousarray(scaled.reshape(k // 512, 128, 4, n).transpose(0, 1, 3, 2))
    if fmt == "e4m3":
        words = by_word.astype(ml_dtypes.float8_e4m3fn).view(np.uint8)
    else:
        c = by_word.astype(ml_dtypes.float4_e2m1fn).view(np.uint8) & 0xF
        words = (c[..., 0::2] | (c[..., 1::2] << 4)).reshape(k // 512, 128, 2 * n)
    return np.ascontiguousarray(words), np.ascontiguousarray(byte.astype(np.uint8).reshape(k // 512, 16, n))


def unpack_weight(words, scales, fmt):
    g, _, n = scales.shape
    words = np.ascontiguousarray(words).reshape(g, 128, n, -1)
    if fmt == "e4m3":
        vals = words.view(ml_dtypes.float8_e4m3fn).astype(np.float64)
    else:
        nib = np.empty((g, 128, n, 4), np.uint8)
        nib[..., 0::2] = words & 0xF
        nib[..., 1::2] = words >> 4
        vals = E2M1[nib]
    vals = vals * np.repeat(np.exp2(scales.astype(np.float64) - 127.0), 8, axis=1)[..., None]
    return vals.transpose(0, 1, 3, 2).reshape(g * 512, n)


def bf(x):
    return np.asarray(x, np.float32).astype(ml_dtypes.bfloat16)


def planes(Y):
    r, m = Y.shape
    b = f64(bf(Y)).reshape(r // 32, 32, m)
    amax = np.abs(b).max(1)
    byte = np.clip(np.where(amax > 0, np.frexp(amax)[1] - 1 + 127 - 7, 1), 1, 254)
    codes = (b * np.exp2(127.0 - byte)[:, None, :]).reshape(r, m).astype(np.float32).astype(ml_dtypes.float8_e4m3fn).view(np.uint8)
    words = codes.reshape(r // 512, 128, 4, m).transpose(0, 1, 3, 2)
    return np.ascontiguousarray(words), np.ascontiguousarray(byte.astype(np.uint8).reshape(r // 512, 16, m))


K, T, J, L, V, N = 512, 1024, 512, 512, 512, 512


def setup_inputs():
    n = np.random.standard_normal
    idx = np.random.permutation(T)[:J]
    idx2 = np.random.permutation(T)[:J]
    idx3 = np.random.randint(0, V, J)
    fk = mx_kscale(K)
    fl = mx_kscale(L)
    wap = pack_weight(n((K, N)) * 1 / np.sqrt(K) * fk[:, None], "e4m3")
    lap = pack_weight(n((L, V)) / fl[:, None], "e2m1")
    wlp = pack_weight(n((L, N)) * 1 / np.sqrt(L) * fl[:, None], "e4m3")
    return {
        "ea": (n((K, T)) / fk[:, None]).astype(np.float32),
        "wa_words": wap[0],
        "wa_scales": wap[1],
        "la_words": lap[0],
        "la_scales": lap[1],
        "wl_words": wlp[0],
        "wl_scales": wlp[1],
        "offs": striped(idx),
        "offs2": striped(idx2),
        "offs3": striped(idx3),
    }


def reference(ea, wa_words, wa_scales, la_words, la_scales, wl_words, wl_scales, offs, offs2, offs3):
    idx = unstriped(offs)
    idx2 = unstriped(offs2)
    idx3 = unstriped(offs3)
    wau = unpack_weight(wa_words, wa_scales, "e4m3")
    lau = unpack_weight(la_words, la_scales, "e2m1")
    wlu = unpack_weight(wl_words, wl_scales, "e4m3")
    d = f64(ea)[:, idx] - 0.5 * f64(ea)[:, idx2]
    dq = mxq(d, 0, "e4m3")
    p = wau.T @ dq
    z = wlu.T @ lau
    y = p * np.maximum(z[:, idx3], 0.0)
    words, scales = planes(y)
    return y, words, scales

@@ -1,0 +1,186 @@
+from contextlib import ExitStack
+
+import concourse.mybir as mybir
+
+K, T, J, L, V, N = 512, 1024, 512, 512, 512, 512
+FLOPS = 2 * K * N * J + 2 * L * N * V
+
+F32 = mybir.dt.float32
+BF16 = mybir.dt.bfloat16
+I32 = mybir.dt.int32
+U16 = mybir.dt.uint16
+U8 = mybir.dt.uint8
+FP8X4 = mybir.dt.float8_e4m3fn_x4
+FP4X4 = mybir.dt.float4_e2m1fn_x4
+ACT = mybir.ActivationFunctionType
+ALU = mybir.AluOpType
+
+P = 128
+PACK = 4
+CHUNKS = [(0, 128), (128, 256), (256, 384), (384, 512)]
+FIRST = 128
+
+
+def tile_list_early_and_late_tables_pl_kernel(
+    tc, ea, wa_words, wa_scales, la_words, la_scales, wl_words, wl_scales, offs, offs2, offs3, out_0, out_1, out_2
+):
+    nc = tc.nc
+    ea_planes = ea.rearrange("(p t) c -> p t c", t=PACK)
+    y_rows = out_0.rearrange("(p t) j -> p t j", t=PACK)
+    code_words = out_1[0].rearrange("p c t -> p (c t)").bitcast(I32)
+
+    def words_of(w):
+        return w[0].rearrange("p n t -> p (n t)").bitcast(I32)
+
+    def cols16(lo, hi):
+        return slice(lo // 16, hi // 16)
+
+    with ExitStack() as ctx:
+        lists = ctx.enter_context(tc.tile_pool(name="lists", bufs=1))
+        keep = ctx.enter_context(tc.tile_pool(name="keep", bufs=1))
+        psum = ctx.enter_context(tc.psum_pool(name="psum", bufs=1))
+
+        list1 = lists.tile([P, J // 16], U16, name="list1")
+        list2 = lists.tile([P, J // 16], U16, name="list2")
+        list3 = lists.tile([P, J // 16], U16, name="list3")
+        plane = [keep.tile([P, T], F32, name="plane%d" % t) for t in range(PACK)]
+        wa_raw = keep.tile([P, N], I32, name="wa_raw")
+        wl_raw = keep.tile([P, N], I32, name="wl_raw")
+        la = keep.tile([P, 2 * V], U8, name="la", align_bytes=64)
+        w_scale_raw = keep.tile([P, N], U8, name="w_scale_raw")
+        la_scale = keep.tile([P, V], U8, name="la_scale", align_bytes=64)
+
+        nc.vector.memset(w_scale_raw[:].bitcast(I32), 0)
+        nc.vector.memset(la_scale[:].bitcast(I32), 0)
+
+        def load_scale_rows(queue, tile, first_row, src):
+            for q in range(4):
+                queue.dma_start(
+                    out=tile[32 * q + first_row : 32 * q + first_row + 4, :].bitcast(I32),
+                    in_=src[0, 4 * q : 4 * q + 4, :].bitcast(I32),
+                )
+
+        nc.sync.dma_start(list2[:], offs2)
+        nc.sync.dma_start(out=plane[0][:], in_=ea_planes[:, 0, :])
+        nc.sync.dma_start(list1[:], offs)
+        nc.sync.dma_start(out=plane[1][:], in_=ea_planes[:, 1, :])
+        load_scale_rows(nc.scalar, w_scale_raw, 0, wl_scales)
+        load_scale_rows(nc.scalar, w_scale_raw, 4, wa_scales)
+        load_scale_rows(nc.scalar, la_scale, 0, la_scales)
+        nc.sync.dma_start(out=wl_raw[:], in_=words_of(wl_words))
+        nc.sync.dma_start(out=la[:].bitcast(I32), in_=la_words[0].bitcast(I32))
+        nc.sync.dma_start(out=plane[2][:], in_=ea_planes[:, 2, :])
+        nc.sync.dma_start(out=plane[3][:], in_=ea_planes[:, 3, :])
+        nc.sync.dma_start(out=wa_raw[:], in_=words_of(wa_words))
+        nc.sync.dma_start(list3[:], offs3)
+
+        def deal_words(dst, src):
+            nc.vector.tensor_copy(
+                out=dst[:].rearrange("p (t c i) -> p c t i", t=PACK, i=4),
+                in_=src[:].rearrange("p (c i t) -> p c t i", t=PACK, i=4),
+            )
+
+        def interleave(dst, src):
+            nc.scalar.activation(
+                out=dst.rearrange("p (c i t) -> p c t i", t=PACK, i=4),
+                in_=src.rearrange("p (t c i) -> p c t i", t=PACK, i=4),
+                func=ACT.Copy,
+            )
+
+        half = [keep.tile([P, J], F32, name="half%d" % t) for t in range(PACK)]
+        d_first = keep.tile([P, PACK * FIRST], F32, name="d_first", tag="even")
+        minus_half = keep.tile([P, J], F32, name="minus_half", tag="odd")
+        nc.gpsimd.memset(minus_half[:], -0.5)
+
+        def gather_half(t, lo, hi):
+            nc.vector.tensor_tensor(
+                half[t][:, lo:hi], plane[t][:].indirect(list2[:, cols16(lo, hi)]), minus_half[:, lo:hi], ALU.mult
+            )
+
+        def gather_diff(dst, t, lo, hi):
+            nc.vector.tensor_tensor(dst, plane[t][:].indirect(list1[:, cols16(lo, hi)]), half[t][:, lo:hi], ALU.add)
+
+        wl = keep.tile([P, N], I32, name="wl", align_bytes=64)
+        wa = keep.tile([P, N], I32, name="wa", align_bytes=64)
+        w_scale = keep.tile([P, N], U8, name="w_scale", align_bytes=64)
+        z_pos = [keep.tile([P, V], F32, name="z_pos%d" % t) for t in range(PACK)]
+
+        for t in range(PACK):
+            gather_half(t, 0, FIRST)
+            gather_half(t, FIRST, J)
+            gather_diff(d_first[:, t * FIRST : (t + 1) * FIRST], t, 0, FIRST)
+            if t == 1:
+                deal_words(wl, wl_raw)
+                nc.vector.tensor_copy(
+                    out=w_scale[:].rearrange("p (t m) -> p t m", t=PACK),
+                    in_=w_scale_raw[:].rearrange("p (m t) -> p t m", t=PACK),
+                )
+                for s in range(PACK):
+                    z_bank = psum.tile([P, V], F32, name="z_bank%d" % s)
+                    nc.tensor.matmul_mx(
+                        out=z_bank[:],
+                        lhsT=wl[:, s * P : (s + 1) * P].bitcast(FP8X4),
+                        lhsT_scale=w_scale[:, s * P : (s + 1) * P],
+                        rhs=la[:].bitcast(FP4X4),
+                        rhs_scale=la_scale[:],
+                        start=True,
+                        stop=True,
+                    )
+                    nc.scalar.activation(out=z_pos[s][:], in_=z_bank[:], func=ACT.Relu)
+        deal_words(wa, wa_raw)
+
+        p_sb = {}
+        for c, (lo, hi) in enumerate(CHUNKS):
+            w = hi - lo
+            if c == 0:
+                d = d_first[:]
+            else:
+                d_tile = keep.tile([P, PACK * w], F32, name="d_tile", tag="odd" if c % 2 else "even")
+                d = d_tile[:]
+                for t in range(PACK):
+                    gather_diff(d[:, t * w : (t + 1) * w], t, lo, hi)
+            d_bf = keep.tile([P, PACK * w], BF16, name="d_bf%d" % lo, align_bytes=64)
+            d_codes = keep.tile([P, w], I32, name="d_codes%d" % lo, align_bytes=64)
+            d_scale = keep.tile([P, w], U8, name="d_scale%d" % lo, align_bytes=64)
+            interleave(d_bf[:], d)
+            nc.vector.quantize_mx(out=d_codes[:].bitcast(FP8X4), scales=d_scale[:], in_=d_bf[:])
+            p_sb[lo] = keep.tile([P, PACK * w], F32, name="p_sb%d" % lo)
+            per_bank = 512 // w
+            for b in range(PACK // per_bank):
+                p_bank = psum.tile([P, 512], F32, name="p_bank%d_%d" % (lo, b))
+                for u in range(per_bank):
+                    t = b * per_bank + u
+                    nc.tensor.matmul_mx(
+                        out=p_bank[:, u * w : (u + 1) * w],
+                        lhsT=wa[:, t * P : (t + 1) * P].bitcast(FP8X4),
+                        lhsT_scale=w_scale[4:P, t * P : (t + 1) * P],
+                        rhs=d_codes[:].bitcast(FP8X4),
+                        rhs_scale=d_scale[:],
+                        start=True,
+                        stop=True,
+                    )
+                nc.scalar.copy(out=p_sb[lo][:, b * 512 : (b + 1) * 512], in_=p_bank[:])
+
+        y_scale = keep.tile([P, J], U8, name="y_scale", align_bytes=64)
+        for c, (lo, hi) in enumerate(CHUNKS):
+            w = hi - lo
+            y = keep.tile([P, PACK * w], F32, name="y", tag=["even", "odd", "y2", "y3"][c])
+            y_bf = keep.tile([P, PACK * w], BF16, name="y_bf%d" % lo, align_bytes=64)
+            y_codes = keep.tile([P, w], I32, name="y_codes%d" % lo, align_bytes=64)
+            for t in range(PACK):
+                nc.vector.tensor_tensor(
+                    y[:, t * w : (t + 1) * w],
+                    z_pos[t][:].indirect(list3[:, cols16(lo, hi)]),
+                    p_sb[lo][:, t * w : (t + 1) * w],
+                    ALU.mult,
+                )
+            nc.sync.dma_start(out=y_rows[:, :, lo:hi], in_=y[:].rearrange("p (t j) -> p t j", t=PACK))
+            interleave(y_bf[:], y[:])
+            nc.vector.quantize_mx(out=y_codes[:].bitcast(FP8X4), scales=y_scale[:, lo:hi], in_=y_bf[:])
+            nc.sync.dma_start(out=code_words[:, lo:hi], in_=y_codes[:])
+        for q in range(4):
+            queue = nc.scalar if q % 2 == 0 else nc.sync
+            queue.dma_start(
+                out=out_2[0, 4 * q : 4 * q + 4, :].bitcast(I32),
+                in_=y_scale[32 * q : 32 * q + 4, :].bitcast(I32),
+            )

@@ -19,6 +19,7 @@ P = 128
 PACK = 4
 CHUNKS = [(0, 128), (128, 256), (256, 384), (384, 512)]
 FIRST = 128
+GROUPS = CHUNKS
 
 
 def tile_list_early_and_late_tables_pl_kernel(
@@ -47,32 +48,40 @@ def tile_list_early_and_late_tables_pl_kernel(
         wa_raw = keep.tile([P, N], I32, name="wa_raw")
         wl_raw = keep.tile([P, N], I32, name="wl_raw")
         la = keep.tile([P, 2 * V], U8, name="la", align_bytes=64)
-        w_scale_raw = keep.tile([P, N], U8, name="w_scale_raw")
+        wl_scale_raw = keep.tile([P, N], U8, name="wl_scale_raw")
+        wa_scale_raw = keep.tile([P, N], U8, name="wa_scale_raw")
         la_scale = keep.tile([P, V], U8, name="la_scale", align_bytes=64)
 
-        nc.vector.memset(w_scale_raw[:].bitcast(I32), 0)
+        nc.vector.memset(wl_scale_raw[:].bitcast(I32), 0)
         nc.vector.memset(la_scale[:].bitcast(I32), 0)
+        nc.vector.memset(wa_scale_raw[:].bitcast(I32), 0)
 
-        def load_scale_rows(queue, tile, first_row, src):
+        def load_scale_rows(tile, src):
             for q in range(4):
-                queue.dma_start(
-                    out=tile[32 * q + first_row : 32 * q + first_row + 4, :].bitcast(I32),
+                nc.sync.dma_start(
+                    out=tile[32 * q : 32 * q + 4, :].bitcast(I32),
                     in_=src[0, 4 * q : 4 * q + 4, :].bitcast(I32),
                 )
 
-        nc.sync.dma_start(list2[:], offs2)
         nc.sync.dma_start(out=plane[0][:], in_=ea_planes[:, 0, :])
+        nc.sync.dma_start(list2[:], offs2)
         nc.sync.dma_start(list1[:], offs)
+        load_scale_rows(wl_scale_raw, wl_scales)
         nc.sync.dma_start(out=plane[1][:], in_=ea_planes[:, 1, :])
-        load_scale_rows(nc.scalar, w_scale_raw, 0, wl_scales)
-        load_scale_rows(nc.scalar, w_scale_raw, 4, wa_scales)
-        load_scale_rows(nc.scalar, la_scale, 0, la_scales)
+        nc.sync.dma_start(out=plane[2][:], in_=ea_planes[:, 2, :])
         nc.sync.dma_start(out=wl_raw[:], in_=words_of(wl_words))
         nc.sync.dma_start(out=la[:].bitcast(I32), in_=la_words[0].bitcast(I32))
-        nc.sync.dma_start(out=plane[2][:], in_=ea_planes[:, 2, :])
+        load_scale_rows(la_scale, la_scales)
         nc.sync.dma_start(out=plane[3][:], in_=ea_planes[:, 3, :])
         nc.sync.dma_start(out=wa_raw[:], in_=words_of(wa_words))
+        load_scale_rows(wa_scale_raw, wa_scales)
         nc.sync.dma_start(list3[:], offs3)
+
+        def deal_scales(dst, src):
+            nc.vector.tensor_copy(
+                out=dst[:].rearrange("p (t m) -> p t m", t=PACK),
+                in_=src[:].rearrange("p (m t) -> p t m", t=PACK),
+            )
 
         def deal_words(dst, src):
             nc.vector.tensor_copy(
@@ -102,7 +111,8 @@ def tile_list_early_and_late_tables_pl_kernel(
 
         wl = keep.tile([P, N], I32, name="wl", align_bytes=64)
         wa = keep.tile([P, N], I32, name="wa", align_bytes=64)
-        w_scale = keep.tile([P, N], U8, name="w_scale", align_bytes=64)
+        wl_scale = keep.tile([P, N], U8, name="wl_scale", align_bytes=64)
+        wa_scale = keep.tile([P, N], U8, name="wa_scale", align_bytes=64)
         z_pos = [keep.tile([P, V], F32, name="z_pos%d" % t) for t in range(PACK)]
 
         for t in range(PACK):
@@ -111,16 +121,13 @@ def tile_list_early_and_late_tables_pl_kernel(
             gather_diff(d_first[:, t * FIRST : (t + 1) * FIRST], t, 0, FIRST)
             if t == 1:
                 deal_words(wl, wl_raw)
-                nc.vector.tensor_copy(
-                    out=w_scale[:].rearrange("p (t m) -> p t m", t=PACK),
-                    in_=w_scale_raw[:].rearrange("p (m t) -> p t m", t=PACK),
-                )
+                deal_scales(wl_scale, wl_scale_raw)
                 for s in range(PACK):
                     z_bank = psum.tile([P, V], F32, name="z_bank%d" % s)
                     nc.tensor.matmul_mx(
                         out=z_bank[:],
                         lhsT=wl[:, s * P : (s + 1) * P].bitcast(FP8X4),
-                        lhsT_scale=w_scale[:, s * P : (s + 1) * P],
+                        lhsT_scale=wl_scale[:, s * P : (s + 1) * P],
                         rhs=la[:].bitcast(FP4X4),
                         rhs_scale=la_scale[:],
                         start=True,
@@ -128,8 +135,14 @@ def tile_list_early_and_late_tables_pl_kernel(
                     )
                     nc.scalar.activation(out=z_pos[s][:], in_=z_bank[:], func=ACT.Relu)
         deal_words(wa, wa_raw)
+        deal_scales(wa_scale, wa_scale_raw)
 
-        p_sb = {}
+        p_sb = {lo: keep.tile([P, PACK, hi - lo], F32, name="p_sb%d" % lo) for lo, hi in GROUPS}
+
+        def p_cols(lo, hi):
+            base = max(g for g in p_sb if g <= lo)
+            return p_sb[base][:, :, lo - base : hi - base]
+
         for c, (lo, hi) in enumerate(CHUNKS):
             w = hi - lo
             if c == 0:
@@ -144,7 +157,6 @@ def tile_list_early_and_late_tables_pl_kernel(
             d_scale = keep.tile([P, w], U8, name="d_scale%d" % lo, align_bytes=64)
             interleave(d_bf[:], d)
             nc.vector.quantize_mx(out=d_codes[:].bitcast(FP8X4), scales=d_scale[:], in_=d_bf[:])
-            p_sb[lo] = keep.tile([P, PACK * w], F32, name="p_sb%d" % lo)
             per_bank = 512 // w
             for b in range(PACK // per_bank):
                 p_bank = psum.tile([P, 512], F32, name="p_bank%d_%d" % (lo, b))
@@ -153,30 +165,44 @@ def tile_list_early_and_late_tables_pl_kernel(
                     nc.tensor.matmul_mx(
                         out=p_bank[:, u * w : (u + 1) * w],
                         lhsT=wa[:, t * P : (t + 1) * P].bitcast(FP8X4),
-                        lhsT_scale=w_scale[4:P, t * P : (t + 1) * P],
+                        lhsT_scale=wa_scale[:, t * P : (t + 1) * P],
                         rhs=d_codes[:].bitcast(FP8X4),
                         rhs_scale=d_scale[:],
                         start=True,
                         stop=True,
                     )
-                nc.scalar.copy(out=p_sb[lo][:, b * 512 : (b + 1) * 512], in_=p_bank[:])
+                nc.scalar.copy(
+                    out=p_cols(lo, hi)[:, b * per_bank : (b + 1) * per_bank, :],
+                    in_=p_bank[:].rearrange("p (u j) -> p u j", u=per_bank),
+                )
 
         y_scale = keep.tile([P, J], U8, name="y_scale", align_bytes=64)
         for c, (lo, hi) in enumerate(CHUNKS):
             w = hi - lo
-            y = keep.tile([P, PACK * w], F32, name="y", tag=["even", "odd", "y2", "y3"][c])
+            y = keep.tile([P, PACK, w], F32, name="y", tag=["even", "odd", "y2", "y3"][c])
             y_bf = keep.tile([P, PACK * w], BF16, name="y_bf%d" % lo, align_bytes=64)
             y_codes = keep.tile([P, w], I32, name="y_codes%d" % lo, align_bytes=64)
-            for t in range(PACK):
-                nc.vector.tensor_tensor(
-                    y[:, t * w : (t + 1) * w],
-                    z_pos[t][:].indirect(list3[:, cols16(lo, hi)]),
-                    p_sb[lo][:, t * w : (t + 1) * w],
-                    ALU.mult,
+            step = w if hi < J else w // 2
+            for a in range(0, w, step):
+                for t in range(PACK):
+                    nc.vector.tensor_tensor(
+                        y[:, t, a : a + step],
+                        z_pos[t][:].indirect(list3[:, cols16(lo + a, lo + a + step)]),
+                        p_sb[lo][:, t, a : a + step],
+                        ALU.mult,
+                    )
+                if a + step == w:
+                    nc.sync.dma_start(out=y_rows[:, :, lo:hi], in_=y[:])
+                nc.scalar.activation(
+                    out=y_bf[:, PACK * a : PACK * (a + step)].rearrange("p (c i t) -> p c t i", t=PACK, i=4),
+                    in_=y[:, :, a : a + step].rearrange("p t (c i) -> p c t i", i=4),
+                    func=ACT.Copy,
                 )
-            nc.sync.dma_start(out=y_rows[:, :, lo:hi], in_=y[:].rearrange("p (t j) -> p t j", t=PACK))
-            interleave(y_bf[:], y[:])
-            nc.vector.quantize_mx(out=y_codes[:].bitcast(FP8X4), scales=y_scale[:, lo:hi], in_=y_bf[:])
+                nc.vector.quantize_mx(
+                    out=y_codes[:, a : a + step].bitcast(FP8X4),
+                    scales=y_scale[:, lo + a : lo + a + step],
+                    in_=y_bf[:, PACK * a : PACK * (a + step)],
+                )
             nc.sync.dma_start(out=code_words[:, lo:hi], in_=y_codes[:])
         for q in range(4):
             queue = nc.scalar if q % 2 == 0 else nc.sync

from contextlib import ExitStack

import concourse.mybir as mybir

K, T, J, L, V, N = 512, 1024, 512, 512, 512, 512
FLOPS = 2 * K * N * J + 2 * L * N * V

F32 = mybir.dt.float32
BF16 = mybir.dt.bfloat16
I32 = mybir.dt.int32
U16 = mybir.dt.uint16
U8 = mybir.dt.uint8
FP8X4 = mybir.dt.float8_e4m3fn_x4
FP4X4 = mybir.dt.float4_e2m1fn_x4
ACT = mybir.ActivationFunctionType
ALU = mybir.AluOpType

P = 128
PACK = 4
CHUNKS = [(0, 128), (128, 256), (256, 384), (384, 512)]
FIRST = 128
GROUPS = CHUNKS


def tile_list_early_and_late_tables_pl_kernel(
    tc, ea, wa_words, wa_scales, la_words, la_scales, wl_words, wl_scales, offs, offs2, offs3, out_0, out_1, out_2
):
    nc = tc.nc
    ea_planes = ea.rearrange("(p t) c -> p t c", t=PACK)
    y_rows = out_0.rearrange("(p t) j -> p t j", t=PACK)
    code_words = out_1[0].rearrange("p c t -> p (c t)").bitcast(I32)

    def words_of(w):
        return w[0].rearrange("p n t -> p (n t)").bitcast(I32)

    def cols16(lo, hi):
        return slice(lo // 16, hi // 16)

    with ExitStack() as ctx:
        lists = ctx.enter_context(tc.tile_pool(name="lists", bufs=1))
        keep = ctx.enter_context(tc.tile_pool(name="keep", bufs=1))
        psum = ctx.enter_context(tc.psum_pool(name="psum", bufs=1))

        list1 = lists.tile([P, J // 16], U16, name="list1")
        list2 = lists.tile([P, J // 16], U16, name="list2")
        list3 = lists.tile([P, J // 16], U16, name="list3")
        plane = [keep.tile([P, T], F32, name="plane%d" % t) for t in range(PACK)]
        wa_raw = keep.tile([P, N], I32, name="wa_raw")
        wl_raw = keep.tile([P, N], I32, name="wl_raw")
        la = keep.tile([P, 2 * V], U8, name="la", align_bytes=64)
        wl_scale_raw = keep.tile([P, N], U8, name="wl_scale_raw")
        wa_scale_raw = keep.tile([P, N], U8, name="wa_scale_raw")
        la_scale = keep.tile([P, V], U8, name="la_scale", align_bytes=64)

        nc.vector.memset(wl_scale_raw[:].bitcast(I32), 0)
        nc.vector.memset(la_scale[:].bitcast(I32), 0)
        nc.vector.memset(wa_scale_raw[:].bitcast(I32), 0)

        def load_scale_rows(tile, src):
            for q in range(4):
                nc.sync.dma_start(
                    out=tile[32 * q : 32 * q + 4, :].bitcast(I32),
                    in_=src[0, 4 * q : 4 * q + 4, :].bitcast(I32),
                )

        nc.sync.dma_start(out=plane[0][:], in_=ea_planes[:, 0, :])
        nc.sync.dma_start(list2[:], offs2)
        nc.sync.dma_start(list1[:], offs)
        load_scale_rows(wl_scale_raw, wl_scales)
        nc.sync.dma_start(out=plane[1][:], in_=ea_planes[:, 1, :])
        nc.sync.dma_start(out=plane[2][:], in_=ea_planes[:, 2, :])
        nc.sync.dma_start(out=wl_raw[:], in_=words_of(wl_words))
        nc.sync.dma_start(out=la[:].bitcast(I32), in_=la_words[0].bitcast(I32))
        load_scale_rows(la_scale, la_scales)
        nc.sync.dma_start(out=plane[3][:], in_=ea_planes[:, 3, :])
        nc.sync.dma_start(out=wa_raw[:], in_=words_of(wa_words))
        load_scale_rows(wa_scale_raw, wa_scales)
        nc.sync.dma_start(list3[:], offs3)

        def deal_scales(dst, src):
            nc.vector.tensor_copy(
                out=dst[:].rearrange("p (t m) -> p t m", t=PACK),
                in_=src[:].rearrange("p (m t) -> p t m", t=PACK),
            )

        def deal_words(dst, src):
            nc.vector.tensor_copy(
                out=dst[:].rearrange("p (t c i) -> p c t i", t=PACK, i=4),
                in_=src[:].rearrange("p (c i t) -> p c t i", t=PACK, i=4),
            )

        def interleave(dst, src):
            nc.scalar.activation(
                out=dst.rearrange("p (c i t) -> p c t i", t=PACK, i=4),
                in_=src.rearrange("p (t c i) -> p c t i", t=PACK, i=4),
                func=ACT.Copy,
            )

        half = [keep.tile([P, J], F32, name="half%d" % t) for t in range(PACK)]
        d_first = keep.tile([P, PACK * FIRST], F32, name="d_first", tag="even")
        minus_half = keep.tile([P, J], F32, name="minus_half", tag="odd")
        nc.gpsimd.memset(minus_half[:], -0.5)

        def gather_half(t, lo, hi):
            nc.vector.tensor_tensor(
                half[t][:, lo:hi], plane[t][:].indirect(list2[:, cols16(lo, hi)]), minus_half[:, lo:hi], ALU.mult
            )

        def gather_diff(dst, t, lo, hi):
            nc.vector.tensor_tensor(dst, plane[t][:].indirect(list1[:, cols16(lo, hi)]), half[t][:, lo:hi], ALU.add)

        wl = keep.tile([P, N], I32, name="wl", align_bytes=64)
        wa = keep.tile([P, N], I32, name="wa", align_bytes=64)
        wl_scale = keep.tile([P, N], U8, name="wl_scale", align_bytes=64)
        wa_scale = keep.tile([P, N], U8, name="wa_scale", align_bytes=64)
        z_pos = [keep.tile([P, V], F32, name="z_pos%d" % t) for t in range(PACK)]

        for t in range(PACK):
            gather_half(t, 0, FIRST)
            gather_half(t, FIRST, J)
            gather_diff(d_first[:, t * FIRST : (t + 1) * FIRST], t, 0, FIRST)
            if t == 1:
                deal_words(wl, wl_raw)
                deal_scales(wl_scale, wl_scale_raw)
                for s in range(PACK):
                    z_bank = psum.tile([P, V], F32, name="z_bank%d" % s)
                    nc.tensor.matmul_mx(
                        out=z_bank[:],
                        lhsT=wl[:, s * P : (s + 1) * P].bitcast(FP8X4),
                        lhsT_scale=wl_scale[:, s * P : (s + 1) * P],
                        rhs=la[:].bitcast(FP4X4),
                        rhs_scale=la_scale[:],
                        start=True,
                        stop=True,
                    )
                    nc.scalar.activation(out=z_pos[s][:], in_=z_bank[:], func=ACT.Relu)
        deal_words(wa, wa_raw)
        deal_scales(wa_scale, wa_scale_raw)

        p_sb = {lo: keep.tile([P, PACK, hi - lo], F32, name="p_sb%d" % lo) for lo, hi in GROUPS}

        def p_cols(lo, hi):
            base = max(g for g in p_sb if g <= lo)
            return p_sb[base][:, :, lo - base : hi - base]

        for c, (lo, hi) in enumerate(CHUNKS):
            w = hi - lo
            if c == 0:
                d = d_first[:]
            else:
                d_tile = keep.tile([P, PACK * w], F32, name="d_tile", tag="odd" if c % 2 else "even")
                d = d_tile[:]
                for t in range(PACK):
                    gather_diff(d[:, t * w : (t + 1) * w], t, lo, hi)
            d_bf = keep.tile([P, PACK * w], BF16, name="d_bf%d" % lo, align_bytes=64)
            d_codes = keep.tile([P, w], I32, name="d_codes%d" % lo, align_bytes=64)
            d_scale = keep.tile([P, w], U8, name="d_scale%d" % lo, align_bytes=64)
            interleave(d_bf[:], d)
            nc.vector.quantize_mx(out=d_codes[:].bitcast(FP8X4), scales=d_scale[:], in_=d_bf[:])
            per_bank = 512 // w
            for b in range(PACK // per_bank):
                p_bank = psum.tile([P, 512], F32, name="p_bank%d_%d" % (lo, b))
                for u in range(per_bank):
                    t = b * per_bank + u
                    nc.tensor.matmul_mx(
                        out=p_bank[:, u * w : (u + 1) * w],
                        lhsT=wa[:, t * P : (t + 1) * P].bitcast(FP8X4),
                        lhsT_scale=wa_scale[:, t * P : (t + 1) * P],
                        rhs=d_codes[:].bitcast(FP8X4),
                        rhs_scale=d_scale[:],
                        start=True,
                        stop=True,
                    )
                nc.scalar.copy(
                    out=p_cols(lo, hi)[:, b * per_bank : (b + 1) * per_bank, :],
                    in_=p_bank[:].rearrange("p (u j) -> p u j", u=per_bank),
                )

        y_scale = keep.tile([P, J], U8, name="y_scale", align_bytes=64)
        for c, (lo, hi) in enumerate(CHUNKS):
            w = hi - lo
            y = keep.tile([P, PACK, w], F32, name="y", tag=["even", "odd", "y2", "y3"][c])
            y_bf = keep.tile([P, PACK * w], BF16, name="y_bf%d" % lo, align_bytes=64)
            y_codes = keep.tile([P, w], I32, name="y_codes%d" % lo, align_bytes=64)
            step = w if hi < J else w // 2
            for a in range(0, w, step):
                for t in range(PACK):
                    nc.vector.tensor_tensor(
                        y[:, t, a : a + step],
                        z_pos[t][:].indirect(list3[:, cols16(lo + a, lo + a + step)]),
                        p_sb[lo][:, t, a : a + step],
                        ALU.mult,
                    )
                if a + step == w:
                    nc.sync.dma_start(out=y_rows[:, :, lo:hi], in_=y[:])
                nc.scalar.activation(
                    out=y_bf[:, PACK * a : PACK * (a + step)].rearrange("p (c i t) -> p c t i", t=PACK, i=4),
                    in_=y[:, :, a : a + step].rearrange("p t (c i) -> p c t i", i=4),
                    func=ACT.Copy,
                )
                nc.vector.quantize_mx(
                    out=y_codes[:, a : a + step].bitcast(FP8X4),
                    scales=y_scale[:, lo + a : lo + a + step],
                    in_=y_bf[:, PACK * a : PACK * (a + step)],
                )
            nc.sync.dma_start(out=code_words[:, lo:hi], in_=y_codes[:])
        for q in range(4):
            queue = nc.scalar if q % 2 == 0 else nc.sync
            queue.dma_start(
                out=out_2[0, 4 * q : 4 * q + 4, :].bitcast(I32),
                in_=y_scale[32 * q : 32 * q + 4, :].bitcast(I32),
            )
